import numpy as np
import ml_dtypes


def mxq(x, axis, fmt="e4m3"):
    dtype, down = {"e4m3": (ml_dtypes.float8_e4m3fn, 7), "e5m2": (ml_dtypes.float8_e5m2, 14)}[fmt]
    v = np.moveaxis(np.asarray(x, np.float32).astype(ml_dtypes.bfloat16).astype(np.float64), axis, -1)
    blocks = v.reshape(v.shape[:-1] + (-1, 32))
    amax = np.abs(blocks).max(-1, keepdims=True)
    byte = np.maximum(np.where(amax > 0, np.frexp(amax)[1] - 1 + 127, 0) - down, 1)
    scale = np.exp2(byte - 127.0)
    codes = (blocks / scale).astype(np.float32).astype(dtype).astype(np.float64)
    return np.moveaxis((codes * scale).reshape(v.shape), -1, axis)


WIDE = False


def mx_kscale(k):
    if not WIDE:
        return np.ones(k)
    levels = np.array([10, -10, 5, -5, 0])
    if k % 512:
        return np.exp2(np.random.permutation(np.resize(levels, k // 32))).repeat(32)
    a = np.empty((k // 512, 16))
    for p in range(k // 512):
        a[p, :8] = np.random.permutation(np.resize(levels, 8))
        for g in range(8):
            far = levels[np.abs(levels - a[p, g]) >= 10]
            a[p, g + 8] = far[np.random.randint(len(far))]
    return np.exp2(a.ravel()).repeat(32)


BF16 = ml_dtypes.bfloat16


def bf(x):
    return np.asarray(x, np.float32).astype(BF16)


def f64(x):
    return np.asarray(x).astype(np.float64)


E2M1 = np.array([0.0, 0.5, 1.0, 1.5, 2.0, 3.0, 4.0, 6.0, -0.0, -0.5, -1.0, -1.5, -2.0, -3.0, -4.0, -6.0])


def pack_weight(w, fmt):
    k, n = w.shape
    w = f64(bf(w)).reshape(k // 32, 32, n)
    amax = np.abs(w).max(1)
    if fmt == "e4m3":
        byte = np.frexp(amax)[1] - 1 + 127 - 7
    else:
        mant, ex = np.frexp(amax / 6.0)
        byte = np.where(mant > 0.5, ex, ex - 1) + 127
    byte = np.clip(np.where(amax > 0, byte, 1), 1, 254)
    scaled = (w * np.exp2(127.0 - byte)[:, None, :]).reshape(k, n).astype(np.float32)
    by_word = np.ascontiguousarray(scaled.reshape(k // 512, 128, 4, n).transpose(0, 1, 3, 2))
    if fmt == "e4m3":
        words = by_word.astype(ml_dtypes.float8_e4m3fn).view(np.uint8)
    else:
        c = by_word.astype(ml_dtypes.float4_e2m1fn).view(np.uint8) & 0xF
        words = c[..., 0::2] | (c[..., 1::2] << 4)
    return np.ascontiguousarray(words), np.ascontiguousarray(byte.astype(np.uint8).reshape(k // 512, 16, n))


def unpack_weight(words, scales, fmt):
    g, p, n, _ = words.shape
    if fmt == "e4m3":
        vals = np.ascontiguousarray(words).view(ml_dtypes.float8_e4m3fn).astype(np.float64)
    else:
        nib = np.empty((g, p, n, 4), np.uint8)
        nib[..., 0::2] = words & 0xF
        nib[..., 1::2] = words >> 4
        vals = E2M1[nib]
    vals = vals * np.repeat(np.exp2(scales.astype(np.float64) - 127.0), 8, axis=1)[..., None]
    return vals.transpose(0, 1, 3, 2).reshape(g * 512, n)
def pack4(w):
    words, scales = pack_weight(w, "e2m1")
    return words.reshape(words.shape[0], 128, -1), scales


def unpack4(words, scales):
    return unpack_weight(words.reshape(words.shape[0], 128, -1, 2), scales, "e2m1")


def planes(Y):
    n, m = Y.shape
    b = f64(bf(Y)).reshape(n // 32, 32, m)
    amax = np.abs(b).max(1)
    byte = np.clip(np.where(amax > 0, np.frexp(amax)[1] - 1 + 127 - 7, 1), 1, 254)
    codes = (b * np.exp2(127.0 - byte)[:, None, :]).reshape(n, m).astype(np.float32).astype(ml_dtypes.float8_e4m3fn).view(np.uint8)
    words = codes.reshape(n // 512, 128, 4, m).transpose(0, 1, 3, 2)
    return np.ascontiguousarray(words), np.ascontiguousarray(byte.astype(np.uint8).reshape(n // 512, 16, m))


M, N, E, K = 1024, 1536, 512, 2048

def setup_inputs():
    s = mx_kscale(E)
    t = mx_kscale(K)
    fingerprint = np.random.randn(M, K) * t
    shape = np.random.randn(M, E) * s
    ref_shape = 0.8 * np.random.randn(N, E) / np.sqrt(E) / s
    mapped = 0.8 * np.random.randn(K, N) / np.sqrt(K) / t[:, None]
    metric_words, metric_scales = pack4(mapped)
    inv_size = np.exp(0.3 * np.random.randn(M))
    ref_weight = np.exp(0.8 * np.random.randn(N))
    return {"fingerprint": bf(fingerprint), "shape": bf(shape),
            "ref_shape": bf(ref_shape), "metric_words": metric_words,
            "metric_scales": metric_scales, "inv_size": bf(inv_size),
            "ref_weight": bf(ref_weight)}

def reference(fingerprint, shape, ref_shape, metric_words, metric_scales, inv_size, ref_weight):
    P = mxq(f64(shape), 1, "e4m3")
    R = mxq(f64(ref_shape), 1, "e4m3")
    overlap = P @ R.T
    X = mxq(f64(fingerprint), 1, "e4m3")
    D = unpack4(metric_words, metric_scales)
    bilinear = X @ D
    y = f64(ref_weight)[None, :] * np.tanh(f64(inv_size)[:, None] * (overlap + bilinear))
    Y = y.T
    words, scales = planes(Y)
    return y, words, scales

@@ -1,0 +1,331 @@
+from contextlib import ExitStack
+
+import concourse.mybir as mybir
+from concourse.masks import make_identity
+
+M, N, E, K = 1024, 1536, 512, 2048
+FLOPS = 2 * M * N * (E + K)
+
+F32 = mybir.dt.float32
+BF16 = mybir.dt.bfloat16
+I32 = mybir.dt.int32
+U32 = mybir.dt.uint32
+U8 = mybir.dt.uint8
+FP8X4 = mybir.dt.float8_e4m3fn_x4
+FP4X4 = mybir.dt.float4_e2m1fn_x4
+TANH = mybir.ActivationFunctionType.Tanh
+MULT = mybir.AluOpType.mult
+
+P = 128
+CHUNK = 512
+TILES = M // P
+CHUNKS = N // CHUNK
+D_PASSES = K // 512
+
+
+def tile_molecule_metric_scores_g5_kernel(
+    tc, fingerprint, shape, ref_shape, metric_words, metric_scales, inv_size, ref_weight, out_0, out_1, out_2
+):
+    nc = tc.nc
+    with ExitStack() as ctx:
+        keep = ctx.enter_context(tc.tile_pool(name="keep", bufs=1))
+        work = ctx.enter_context(tc.tile_pool(name="work", bufs=3))
+        psum = ctx.enter_context(tc.psum_pool(name="psum", bufs=4))
+        ctx.enter_context(tc.manual_schedule(engines={mybir.EngineType.PE, mybir.EngineType.SP}))
+
+        w_words = keep.tile([P, CHUNKS, 4], BF16)
+        nc.scalar.dma_start(out=w_words[:], in_=ref_weight.rearrange("(c p t) -> p c t", p=P, t=4))
+        inv_bf = keep.tile([TILES, P], BF16)
+        nc.scalar.dma_start(out=inv_bf[:], in_=inv_size.rearrange("(t p) -> t p", p=P))
+
+        ident = keep.tile([P, P], F32)
+        make_identity(nc, ident[:])
+        warm = keep.tile([P, 8], F32)
+        nc.scalar.activation(out=warm[:, 0:1], in_=ident[:, 0:1], func=TANH)
+
+        d_words = [keep.tile([P, D_PASSES, 2 * CHUNK], U8, name="d_words%d" % c, align_bytes=256) for c in range(CHUNKS)]
+        d_scales = [keep.tile([P, D_PASSES, CHUNK], U8, name="d_scales%d" % c, align_bytes=256) for c in range(CHUNKS)]
+        for c in range(CHUNKS):
+            nc.vector.memset(d_scales[c][:].bitcast(I32), 0)
+
+        fp_raw = [keep.tile([P, K], BF16, name="fp_raw%d" % t) for t in range(TILES)]
+        sh_raw = [keep.tile([P, 2 * E], BF16, name="sh_raw%d" % h) for h in range(TILES // 2)]
+        r_raw = [keep.tile([P, 2, 2 * E], BF16, name="r_raw%d" % c) for c in range(CHUNKS)]
+
+        def load_fp(t, parts=1):
+            width = K // parts
+            for a in range(0, K, width):
+                nc.sync.dma_start(out=fp_raw[t][:, a : a + width], in_=fingerprint[t * P : (t + 1) * P, a : a + width])
+
+        def load_sh(h):
+            rows = shape[2 * P * h : 2 * P * (h + 1), :]
+            nc.sync.dma_start(out=sh_raw[h][:], in_=rows.rearrange("(r b) k -> r (b k)", b=2))
+
+        def load_r(c):
+            rows = ref_shape[CHUNK * c : CHUNK * (c + 1), :]
+            nc.sync.dma_start(out=r_raw[c][:], in_=rows.rearrange("(h r b) k -> r h (b k)", h=2, b=2))
+
+        def load_d(c):
+            src = metric_words[:, :, 2 * CHUNK * c : 2 * CHUNK * (c + 1)].rearrange("g p b -> p g b")
+            nc.sync.dma_start(out=d_words[c][:].bitcast(I32), in_=src.bitcast(I32))
+            for q in range(4):
+                rows = metric_scales[:, 4 * q : 4 * q + 4, CHUNK * c : CHUNK * (c + 1)].rearrange("g r n -> r g n")
+                nc.sync.dma_start(out=d_scales[c][32 * q : 32 * q + 4, :, :].bitcast(I32), in_=rows.bitcast(I32))
+
+        load_fp(0, parts=2)
+        load_fp(1)
+        load_d(0)
+        load_sh(0)
+        load_r(0)
+        load_d(1)
+        load_r(1)
+        load_fp(2)
+        load_d(2)
+        load_r(2)
+        load_sh(1)
+        load_fp(3)
+        load_fp(4)
+        load_sh(2)
+        load_fp(5)
+        load_fp(6)
+        load_sh(3)
+        load_fp(7)
+
+        fp_codes = keep.tile([P, TILES, D_PASSES * P], U32, align_bytes=256)
+        fp_scales = keep.tile([P, TILES, D_PASSES * P], U8, align_bytes=256)
+        sh_codes = keep.tile([P, M], U32, align_bytes=256)
+        sh_scales = keep.tile([P, M], U8, align_bytes=256)
+        r_codes = keep.tile([P, N], U32, align_bytes=256)
+        r_scales = keep.tile([P, N], U8, align_bytes=256)
+        y_codes = keep.tile([P, CHUNKS, M], U32, align_bytes=256)
+        y_scales = keep.tile([P, CHUNKS, M], U8, align_bytes=256)
+        w_rows = keep.tile([P, N], BF16)
+        inv_rows = keep.tile([P, P], F32)
+        inv_cols = keep.tile([P, TILES], F32)
+
+        def halves_in_place(words):
+            return [words[:, u : 2 * P : 2] for u in range(2)]
+
+        def split_words(raw, count):
+            split = work.tile([P, count, 2, P], F32, tag="split%d" % count)
+            nc.vector.tensor_copy(out=split[:], in_=raw.bitcast(F32).rearrange("p (s c u) -> p s u c", u=2, c=P))
+            return [[split[:, s, u, :] for u in range(2)] for s in range(count)]
+
+        def transpose_bank(stretches):
+            bank = psum.tile([P, 2, 2, P], F32, tag="turn")
+            for s, halves in enumerate(stretches):
+                for u in range(2):
+                    nc.tensor.transpose(bank[:, s, u, :], halves[u], ident[:])
+            return bank
+
+        def quantise(bank, count, order, targets):
+            grouped = work.tile([P, 2 * 4 * P], BF16, tag="grouped", bufs=6, align_bytes=64)
+            words = grouped[:, : count * 4 * P].bitcast(F32)
+            if order == "stretch":
+                nc.scalar.copy(
+                    out=words.rearrange("p (s r u) -> p s r u", s=count, u=2),
+                    in_=bank[:, :count, :, :].rearrange("p s u r -> p s r u"),
+                )
+            else:
+                nc.scalar.copy(
+                    out=words.rearrange("p (r s u) -> p r s u", s=count, u=2),
+                    in_=bank[:, :count, :, :].rearrange("p s u r -> p r s u"),
+                )
+            first = 0
+            for codes, scales in targets:
+                width = 4 * codes.shape[1]
+                nc.vector.quantize_mx(out=codes.bitcast(FP8X4), scales=scales, in_=grouped[:, first : first + width])
+                first += width
+
+        fp_halves = {}
+        sh_halves = {}
+        r_halves = {}
+        y_halves = {}
+        acc = {}
+
+        def split_fp(t):
+            fp_halves[t] = split_words(fp_raw[t][:], D_PASSES)
+
+        def split_sh(h):
+            sh_halves[h] = split_words(sh_raw[h][:], 2)
+
+        def split_r(c):
+            r_halves[c] = split_words(r_raw[c][:].rearrange("p h k -> p (h k)"), 4)
+
+        def turn(*jobs):
+            banks = [transpose_bank(job[0]) for job in jobs]
+            for bank, job in zip(banks, jobs):
+                quantise(bank, len(job[0]), job[1], job[2])
+
+        def fp_jobs(t):
+            jobs = []
+            for g in (0, 2):
+                cols = slice(g * P, (g + 2) * P)
+                jobs.append((fp_halves[t][g : g + 2], "stretch", [(fp_codes[:, t, cols], fp_scales[:, t, cols])]))
+            return jobs
+
+        def sh_job(h):
+            cols = slice(2 * P * h, 2 * P * (h + 1))
+            return (sh_halves[h], "row", [(sh_codes[:, cols], sh_scales[:, cols])])
+
+        def r_jobs(c):
+            jobs = []
+            for h in range(2):
+                cols = slice(CHUNK * c + 2 * P * h, CHUNK * c + 2 * P * (h + 1))
+                jobs.append((r_halves[c][2 * h : 2 * h + 2], "row", [(r_codes[:, cols], r_scales[:, cols])]))
+            return jobs
+
+        def y_job(*units):
+            targets = [(y_codes[:, c, t * P : (t + 1) * P], y_scales[:, c, t * P : (t + 1) * P]) for t, c in units]
+            return ([y_halves[pair] for pair in units], "stretch", targets)
+
+        def metric_passes(t, c):
+            acc[t, c] = psum.tile([P, CHUNK], F32, tag="acc", name="acc")
+            for g in range(D_PASSES):
+                cols = slice(g * P, (g + 1) * P)
+                nc.tensor.matmul_mx(
+                    out=acc[t, c][:],
+                    lhsT=fp_codes[:, t, cols].bitcast(FP8X4),
+                    lhsT_scale=fp_scales[:, t, cols],
+                    rhs=d_words[c][:, g, :].bitcast(FP4X4),
+                    rhs_scale=d_scales[c][:, g, :],
+                    start=(g == 0),
+                    stop=False,
+                )
+
+        def finish(t, c, last=False):
+            rows = slice(t * P, (t + 1) * P)
+            cols = slice(c * CHUNK, (c + 1) * CHUNK)
+            nc.tensor.matmul_mx(
+                out=acc[t, c][:],
+                lhsT=sh_codes[:, rows].bitcast(FP8X4),
+                lhsT_scale=sh_scales[:, rows],
+                rhs=r_codes[:, cols].bitcast(FP8X4),
+                rhs_scale=r_scales[:, cols],
+                start=False,
+                stop=True,
+            )
+            squashed = work.tile([P, CHUNK], F32, tag="squashed", bufs=4)
+            nc.scalar.activation(out=squashed[:], in_=acc[t, c][:], func=TANH, scale=inv_cols[:, t : t + 1])
+            y = work.tile([P, CHUNK], F32, tag="y", bufs=12)
+            y_bf = work.tile([P, 2, P, 2], BF16, tag="y_bf", bufs=10)
+            if last:
+                nc.vector.tensor_tensor(
+                    out=y_bf[:],
+                    in0=squashed[:].rearrange("p (c u e) -> p u c e", u=2, e=2),
+                    in1=w_rows[:, cols].rearrange("p (c u e) -> p u c e", u=2, e=2),
+                    op=MULT,
+                )
+                nc.vector.tensor_tensor(out=y[:], in0=squashed[:], in1=w_rows[:, cols], op=MULT)
+            else:
+                nc.vector.tensor_tensor(out=y[:], in0=squashed[:], in1=w_rows[:, cols], op=MULT)
+                nc.vector.tensor_copy(out=y_bf[:], in_=y[:].rearrange("p (c u e) -> p u c e", u=2, e=2))
+            nc.sync.dma_start(out=out_0[rows, cols], in_=y[:])
+            y_halves[t, c] = [y_bf[:, u, :, :].rearrange("p c e -> p (c e)").bitcast(F32) for u in range(2)]
+
+        def unit(t, c, last=False):
+            metric_passes(t, c)
+            finish(t, c, last)
+
+        code_rows = out_1.rearrange("g p m t -> p g (m t)")
+
+        def store_codes(t, groups):
+            nc.sync.dma_start(
+                out=code_rows[:, groups, 4 * P * t : 4 * P * (t + 1)].bitcast(I32),
+                in_=y_codes[:, groups, t * P : (t + 1) * P].bitcast(I32),
+            )
+
+        def store_scales(cols, queues):
+            for q in range(4):
+                queues[q].dma_start(
+                    out=out_2[:, 4 * q : 4 * q + 4, cols].rearrange("g r m -> r g m").bitcast(I32),
+                    in_=y_scales[32 * q : 32 * q + 4, :, cols].bitcast(I32),
+                )
+
+        def constants():
+            nc.gpsimd.memset(inv_rows[:], 0.0)
+            nc.vector.tensor_copy(out=inv_rows[:TILES, :], in_=inv_bf[:])
+            spread = [
+                [w_words[:, c, :].bitcast(F32)[:, u : u + 1].to_broadcast([P, P]) for u in range(2)]
+                for c in range(CHUNKS)
+            ]
+            w_out = w_rows[:].bitcast(F32).rearrange("p (c r u) -> p c r u", c=CHUNKS, u=2)
+            bank_a = transpose_bank(spread[:2])
+            bank_b = transpose_bank(spread[2:])
+            nc.tensor.transpose(bank_b[:, 1, 0, :], inv_rows[:], ident[:])
+            nc.scalar.copy(out=w_out[:, :2, :, :], in_=bank_a[:].rearrange("p s u r -> p s r u"))
+            nc.scalar.copy(out=w_out[:, 2, :, :], in_=bank_b[:, 0, :, :].rearrange("p u r -> p r u"))
+            nc.scalar.copy(out=inv_cols[:], in_=bank_b[:, 1, 0, :TILES])
+
+        for t in range(2):
+            words = fp_raw[t][:].bitcast(F32)
+            fp_halves[t] = [halves_in_place(words[:, 2 * P * g : 2 * P * (g + 1)]) for g in range(D_PASSES)]
+        turn(*fp_jobs(0), *fp_jobs(1))
+        constants()
+        split_sh(0)
+        split_r(0)
+        metric_passes(0, 0)
+        metric_passes(1, 0)
+
+        turn(sh_job(0), *r_jobs(0))
+        split_r(1)
+        split_fp(2)
+        metric_passes(0, 1)
+        metric_passes(1, 1)
+        finish(0, 0)
+        finish(1, 0)
+
+        turn(*r_jobs(1), *fp_jobs(2))
+        split_r(2)
+        split_sh(1)
+        metric_passes(0, 2)
+        metric_passes(1, 2)
+        finish(0, 1)
+        finish(1, 1)
+
+        turn(sh_job(1), *r_jobs(2), y_job((0, 0), (1, 0)))
+        split_fp(3)
+        metric_passes(2, 0)
+        metric_passes(2, 1)
+
+        turn(*fp_jobs(3), y_job((0, 1), (1, 1)))
+        split_fp(4)
+        split_sh(2)
+        finish(0, 2)
+        finish(1, 2)
+        finish(2, 0)
+        finish(2, 1)
+        unit(2, 2)
+
+        waiting = [(0, 2), (1, 2)] + [(t, c) for t in range(2, TILES) for c in range(CHUNKS)]
+        stored = 0
+        for t in range(3, TILES):
+            jobs = []
+            if t + 1 < TILES:
+                jobs += fp_jobs(t + 1)
+            if t in (3, 5):
+                jobs.append(sh_job((t + 1) // 2))
+            y_banks = 1 if t in (3, 5) else 2
+            for b in range(y_banks):
+                jobs.append(y_job(*waiting[:2]))
+                waiting = waiting[2:]
+            turn(*jobs)
+            if t + 2 < TILES:
+                split_fp(t + 2)
+            if t == 4:
+                split_sh(3)
+            while stored < waiting[0][0]:
+                store_codes(stored, slice(0, CHUNKS))
+                stored += 1
+            for c in range(CHUNKS):
+                unit(t, c, last=(t == TILES - 1 and c == CHUNKS - 1))
+
+        last = TILES - 1
+        turn(y_job((last - 1, 2), (last, 0)))
+        store_codes(last - 1, slice(0, CHUNKS))
+        store_scales(slice(0, last * P), [nc.sync] * 4)
+        turn(y_job((last, 1)))
+        store_codes(last, slice(0, 2))
+        turn(y_job((last, 2)))
+        store_codes(last, slice(2, 3))
+        store_scales(slice(last * P, M), [nc.scalar, nc.scalar, nc.sync, nc.sync])

@@ -31,7 +31,7 @@ def tile_molecule_metric_scores_g5_kernel(
         keep = ctx.enter_context(tc.tile_pool(name="keep", bufs=1))
         work = ctx.enter_context(tc.tile_pool(name="work", bufs=3))
         psum = ctx.enter_context(tc.psum_pool(name="psum", bufs=4))
-        ctx.enter_context(tc.manual_schedule(engines={mybir.EngineType.PE, mybir.EngineType.SP}))
+        ctx.enter_context(tc.manual_schedule())
 
         w_words = keep.tile([P, CHUNKS, 4], BF16)
         nc.scalar.dma_start(out=w_words[:], in_=ref_weight.rearrange("(c p t) -> p c t", p=P, t=4))
@@ -52,10 +52,9 @@ def tile_molecule_metric_scores_g5_kernel(
         sh_raw = [keep.tile([P, 2 * E], BF16, name="sh_raw%d" % h) for h in range(TILES // 2)]
         r_raw = [keep.tile([P, 2, 2 * E], BF16, name="r_raw%d" % c) for c in range(CHUNKS)]
 
-        def load_fp(t, parts=1):
-            width = K // parts
-            for a in range(0, K, width):
-                nc.sync.dma_start(out=fp_raw[t][:, a : a + width], in_=fingerprint[t * P : (t + 1) * P, a : a + width])
+        def load_fp(t, first=0, last=D_PASSES):
+            cols = slice(512 * first, 512 * last)
+            nc.sync.dma_start(out=fp_raw[t][:, cols], in_=fingerprint[t * P : (t + 1) * P, cols])
 
         def load_sh(h):
             rows = shape[2 * P * h : 2 * P * (h + 1), :]
@@ -65,25 +64,31 @@ def tile_molecule_metric_scores_g5_kernel(
             rows = ref_shape[CHUNK * c : CHUNK * (c + 1), :]
             nc.sync.dma_start(out=r_raw[c][:], in_=rows.rearrange("(h r b) k -> r h (b k)", h=2, b=2))
 
-        def load_d(c):
-            src = metric_words[:, :, 2 * CHUNK * c : 2 * CHUNK * (c + 1)].rearrange("g p b -> p g b")
-            nc.sync.dma_start(out=d_words[c][:].bitcast(I32), in_=src.bitcast(I32))
+        def load_d_words(c, first=0, last=D_PASSES):
+            src = metric_words[first:last, :, 2 * CHUNK * c : 2 * CHUNK * (c + 1)].rearrange("g p b -> p g b")
+            nc.sync.dma_start(out=d_words[c][:, first:last, :].bitcast(I32), in_=src.bitcast(I32))
+
+        def load_d_scales(c):
             for q in range(4):
                 rows = metric_scales[:, 4 * q : 4 * q + 4, CHUNK * c : CHUNK * (c + 1)].rearrange("g r n -> r g n")
                 nc.sync.dma_start(out=d_scales[c][32 * q : 32 * q + 4, :, :].bitcast(I32), in_=rows.bitcast(I32))
 
-        load_fp(0, parts=2)
+        load_fp(0, 0, 2)
+        load_fp(0, 2, 4)
+        load_d_scales(0)
+        load_d_words(0)
         load_fp(1)
-        load_d(0)
+        load_fp(2)
+        load_fp(3)
         load_sh(0)
         load_r(0)
-        load_d(1)
-        load_r(1)
-        load_fp(2)
-        load_d(2)
-        load_r(2)
         load_sh(1)
-        load_fp(3)
+        load_d_words(1)
+        load_d_scales(1)
+        load_r(1)
+        load_d_words(2)
+        load_d_scales(2)
+        load_r(2)
         load_fp(4)
         load_sh(2)
         load_fp(5)
@@ -103,85 +108,81 @@ def tile_molecule_metric_scores_g5_kernel(
         inv_rows = keep.tile([P, P], F32)
         inv_cols = keep.tile([P, TILES], F32)
 
-        def halves_in_place(words):
-            return [words[:, u : 2 * P : 2] for u in range(2)]
-
-        def split_words(raw, count):
-            split = work.tile([P, count, 2, P], F32, tag="split%d" % count)
-            nc.vector.tensor_copy(out=split[:], in_=raw.bitcast(F32).rearrange("p (s c u) -> p s u c", u=2, c=P))
-            return [[split[:, s, u, :] for u in range(2)] for s in range(count)]
-
-        def transpose_bank(stretches):
-            bank = psum.tile([P, 2, 2, P], F32, tag="turn")
-            for s, halves in enumerate(stretches):
-                for u in range(2):
-                    nc.tensor.transpose(bank[:, s, u, :], halves[u], ident[:])
-            return bank
-
-        def quantise(bank, count, order, targets):
-            grouped = work.tile([P, 2 * 4 * P], BF16, tag="grouped", bufs=6, align_bytes=64)
-            words = grouped[:, : count * 4 * P].bitcast(F32)
-            if order == "stretch":
-                nc.scalar.copy(
-                    out=words.rearrange("p (s r u) -> p s r u", s=count, u=2),
-                    in_=bank[:, :count, :, :].rearrange("p s u r -> p s r u"),
-                )
-            else:
-                nc.scalar.copy(
-                    out=words.rearrange("p (r s u) -> p r s u", s=count, u=2),
-                    in_=bank[:, :count, :, :].rearrange("p s u r -> p r s u"),
-                )
-            first = 0
-            for codes, scales in targets:
-                width = 4 * codes.shape[1]
-                nc.vector.quantize_mx(out=codes.bitcast(FP8X4), scales=scales, in_=grouped[:, first : first + width])
-                first += width
-
-        fp_halves = {}
-        sh_halves = {}
-        r_halves = {}
-        y_halves = {}
+        halves = {}
+        banks = {}
+        staged = {}
         acc = {}
+        squashed = {}
+        y_f32 = {}
+
+        def split(key, raw, count):
+            parted = work.tile([P, count, 2, P], F32, tag="parted%d" % count, name="parted")
+            nc.vector.tensor_copy(out=parted[:], in_=raw.bitcast(F32).rearrange("p (s c u) -> p s u c", u=2, c=P))
+            for s in range(count):
+                halves[key + (s,)] = [parted[:, s, u, :] for u in range(2)]
 
         def split_fp(t):
-            fp_halves[t] = split_words(fp_raw[t][:], D_PASSES)
+            split(("fp", t), fp_raw[t][:], D_PASSES)
 
         def split_sh(h):
-            sh_halves[h] = split_words(sh_raw[h][:], 2)
+            split(("sh", h), sh_raw[h][:], 2)
 
         def split_r(c):
-            r_halves[c] = split_words(r_raw[c][:].rearrange("p h k -> p (h k)"), 4)
+            split(("r", c), r_raw[c][:].rearrange("p h k -> p (h k)"), 4)
 
-        def turn(*jobs):
-            banks = [transpose_bank(job[0]) for job in jobs]
-            for bank, job in zip(banks, jobs):
-                quantise(bank, len(job[0]), job[1], job[2])
+        def unsplit_fp(t):
+            words = fp_raw[t][:].bitcast(F32)
+            for g in range(D_PASSES):
+                halves["fp", t, g] = [words[:, 2 * P * g + u : 2 * P * (g + 1) : 2] for u in range(2)]
 
-        def fp_jobs(t):
-            jobs = []
-            for g in (0, 2):
-                cols = slice(g * P, (g + 2) * P)
-                jobs.append((fp_halves[t][g : g + 2], "stretch", [(fp_codes[:, t, cols], fp_scales[:, t, cols])]))
-            return jobs
+        def fp_job(t, a):
+            cols = slice(2 * a * P, 2 * (a + 1) * P)
+            return (("fp", t, 2 * a), ("fp", t, 2 * a + 1)), "s r u", [(fp_codes[:, t, cols], fp_scales[:, t, cols])]
 
         def sh_job(h):
             cols = slice(2 * P * h, 2 * P * (h + 1))
-            return (sh_halves[h], "row", [(sh_codes[:, cols], sh_scales[:, cols])])
+            return (("sh", h, 0), ("sh", h, 1)), "r s u", [(sh_codes[:, cols], sh_scales[:, cols])]
 
-        def r_jobs(c):
-            jobs = []
-            for h in range(2):
-                cols = slice(CHUNK * c + 2 * P * h, CHUNK * c + 2 * P * (h + 1))
-                jobs.append((r_halves[c][2 * h : 2 * h + 2], "row", [(r_codes[:, cols], r_scales[:, cols])]))
-            return jobs
+        def r_job(c, a):
+            cols = slice(CHUNK * c + 2 * P * a, CHUNK * c + 2 * P * (a + 1))
+            return (("r", c, 2 * a), ("r", c, 2 * a + 1)), "r s u", [(r_codes[:, cols], r_scales[:, cols])]
 
         def y_job(*units):
-            targets = [(y_codes[:, c, t * P : (t + 1) * P], y_scales[:, c, t * P : (t + 1) * P]) for t, c in units]
-            return ([y_halves[pair] for pair in units], "stretch", targets)
+            spans = [(c, t, t + 1) for t, c in units]
+            if len(units) == 2 and units[1] == (units[0][0] + 1, units[0][1]):
+                spans = [(units[0][1], units[0][0], units[0][0] + 2)]
+            targets = [(y_codes[:, c, a * P : b * P], y_scales[:, c, a * P : b * P]) for c, a, b in spans]
+            return tuple(("y",) + pair for pair in units), "s r u", targets
 
-        def metric_passes(t, c):
-            acc[t, c] = psum.tile([P, CHUNK], F32, tag="acc", name="acc")
-            for g in range(D_PASSES):
+        def turn(*jobs):
+            for job in jobs:
+                banks[job[0]] = psum.tile([P, 2, 2, P], F32, tag="turn", name="turn")
+                for s, key in enumerate(job[0]):
+                    for u in range(2):
+                        nc.tensor.transpose(banks[job[0]][:, s, u, :], halves[key][u], ident[:])
+
+        def empty(job):
+            keys, order = job[0], job[1]
+            staged[keys] = work.tile([P, 2 * 4 * P], BF16, tag="staged", name="staged", bufs=6, align_bytes=64)
+            words = staged[keys][:, : len(keys) * 4 * P].bitcast(F32)
+            nc.scalar.copy(
+                out=words.rearrange("p (%s) -> p %s" % (order, order), s=len(keys), u=2),
+                in_=banks[keys][:, : len(keys), :, :].rearrange("p s u r -> p %s" % order),
+            )
+
+        def quantise(job):
+            first = 0
+            for codes, scales in job[2]:
+                width = 4 * codes.shape[1]
+                nc.vector.quantize_mx(
+                    out=codes.bitcast(FP8X4), scales=scales, in_=staged[job[0]][:, first : first + width]
+                )
+                first += width
+
+        def metric_passes(t, c, first=0, last=D_PASSES):
+            if first == 0:
+                acc[t, c] = psum.tile([P, CHUNK], F32, tag="acc", name="acc")
+            for g in range(first, last):
                 cols = slice(g * P, (g + 1) * P)
                 nc.tensor.matmul_mx(
                     out=acc[t, c][:],
@@ -193,7 +194,7 @@ def tile_molecule_metric_scores_g5_kernel(
                     stop=False,
                 )
 
-        def finish(t, c, last=False):
+        def shape_pass(t, c):
             rows = slice(t * P, (t + 1) * P)
             cols = slice(c * CHUNK, (c + 1) * CHUNK)
             nc.tensor.matmul_mx(
@@ -205,127 +206,204 @@ def tile_molecule_metric_scores_g5_kernel(
                 start=False,
                 stop=True,
             )
-            squashed = work.tile([P, CHUNK], F32, tag="squashed", bufs=4)
-            nc.scalar.activation(out=squashed[:], in_=acc[t, c][:], func=TANH, scale=inv_cols[:, t : t + 1])
-            y = work.tile([P, CHUNK], F32, tag="y", bufs=12)
+
+        def unit(t, c):
+            metric_passes(t, c)
+            shape_pass(t, c)
+
+        def squash(t, c):
+            squashed[t, c] = work.tile([P, CHUNK], F32, tag="squashed", name="squashed", bufs=4)
+            nc.scalar.activation(out=squashed[t, c][:], in_=acc[t, c][:], func=TANH, scale=inv_cols[:, t : t + 1])
+
+        def weigh(t, c):
+            cols = slice(c * CHUNK, (c + 1) * CHUNK)
+            y_f32[t, c] = work.tile([P, CHUNK], F32, tag="y", name="y", bufs=12)
+            nc.vector.tensor_tensor(out=y_f32[t, c][:], in0=squashed[t, c][:], in1=w_rows[:, cols], op=MULT)
+            nc.sync.dma_start(out=out_0[t * P : (t + 1) * P, cols], in_=y_f32[t, c][:])
+
+        def round_y(t, c, direct=False):
             y_bf = work.tile([P, 2, P, 2], BF16, tag="y_bf", bufs=10)
-            if last:
+            parted = "p (c u e) -> p u c e"
+            if direct:
                 nc.vector.tensor_tensor(
                     out=y_bf[:],
-                    in0=squashed[:].rearrange("p (c u e) -> p u c e", u=2, e=2),
-                    in1=w_rows[:, cols].rearrange("p (c u e) -> p u c e", u=2, e=2),
+                    in0=squashed[t, c][:].rearrange(parted, u=2, e=2),
+                    in1=w_rows[:, c * CHUNK : (c + 1) * CHUNK].rearrange(parted, u=2, e=2),
                     op=MULT,
                 )
-                nc.vector.tensor_tensor(out=y[:], in0=squashed[:], in1=w_rows[:, cols], op=MULT)
             else:
-                nc.vector.tensor_tensor(out=y[:], in0=squashed[:], in1=w_rows[:, cols], op=MULT)
-                nc.vector.tensor_copy(out=y_bf[:], in_=y[:].rearrange("p (c u e) -> p u c e", u=2, e=2))
-            nc.sync.dma_start(out=out_0[rows, cols], in_=y[:])
-            y_halves[t, c] = [y_bf[:, u, :, :].rearrange("p c e -> p (c e)").bitcast(F32) for u in range(2)]
-
-        def unit(t, c, last=False):
-            metric_passes(t, c)
-            finish(t, c, last)
+                nc.vector.tensor_copy(out=y_bf[:], in_=y_f32[t, c][:].rearrange(parted, u=2, e=2))
+            halves["y", t, c] = [y_bf[:, u, :, :].rearrange("p c e -> p (c e)").bitcast(F32) for u in range(2)]
 
         code_rows = out_1.rearrange("g p m t -> p g (m t)")
 
-        def store_codes(t, groups):
+        def store_codes(first, last, groups=slice(0, CHUNKS)):
             nc.sync.dma_start(
-                out=code_rows[:, groups, 4 * P * t : 4 * P * (t + 1)].bitcast(I32),
-                in_=y_codes[:, groups, t * P : (t + 1) * P].bitcast(I32),
+                out=code_rows[:, groups, 4 * P * first : 4 * P * last].bitcast(I32),
+                in_=y_codes[:, groups, first * P : last * P].bitcast(I32),
             )
 
-        def store_scales(cols, queues):
+        def store_scales(first, last, queues):
+            cols = slice(first * P, last * P)
             for q in range(4):
                 queues[q].dma_start(
                     out=out_2[:, 4 * q : 4 * q + 4, cols].rearrange("g r m -> r g m").bitcast(I32),
                     in_=y_scales[32 * q : 32 * q + 4, :, cols].bitcast(I32),
                 )
 
-        def constants():
-            nc.gpsimd.memset(inv_rows[:], 0.0)
-            nc.vector.tensor_copy(out=inv_rows[:TILES, :], in_=inv_bf[:])
-            spread = [
-                [w_words[:, c, :].bitcast(F32)[:, u : u + 1].to_broadcast([P, P]) for u in range(2)]
-                for c in range(CHUNKS)
-            ]
-            w_out = w_rows[:].bitcast(F32).rearrange("p (c r u) -> p c r u", c=CHUNKS, u=2)
-            bank_a = transpose_bank(spread[:2])
-            bank_b = transpose_bank(spread[2:])
-            nc.tensor.transpose(bank_b[:, 1, 0, :], inv_rows[:], ident[:])
-            nc.scalar.copy(out=w_out[:, :2, :, :], in_=bank_a[:].rearrange("p s u r -> p s r u"))
-            nc.scalar.copy(out=w_out[:, 2, :, :], in_=bank_b[:, 0, :, :].rearrange("p u r -> p r u"))
-            nc.scalar.copy(out=inv_cols[:], in_=bank_b[:, 1, 0, :TILES])
+        def turn_constants():
+            for key, chunks in (("w01", (0, 1)), ("w2", (2,))):
+                banks[key] = psum.tile([P, 2, 2, P], F32, tag="turn", name="turn")
+                for s, c in enumerate(chunks):
+                    for u in range(2):
+                        column = w_words[:, c, :].bitcast(F32)[:, u : u + 1]
+                        nc.tensor.transpose(banks[key][:, s, u, :], column.to_broadcast([P, P]), ident[:])
+            nc.tensor.transpose(banks["w2"][:, 1, 0, :], inv_rows[:], ident[:])
 
-        for t in range(2):
-            words = fp_raw[t][:].bitcast(F32)
-            fp_halves[t] = [halves_in_place(words[:, 2 * P * g : 2 * P * (g + 1)]) for g in range(D_PASSES)]
-        turn(*fp_jobs(0), *fp_jobs(1))
-        constants()
-        split_sh(0)
-        split_r(0)
+        def empty_constants():
+            w_out = w_rows[:].bitcast(F32).rearrange("p (c r u) -> p c r u", c=CHUNKS, u=2)
+            nc.scalar.copy(out=w_out[:, :2, :, :], in_=banks["w01"][:].rearrange("p s u r -> p s r u"))
+            nc.scalar.copy(out=w_out[:, 2, :, :], in_=banks["w2"][:, 0, :, :].rearrange("p u r -> p r u"))
+            nc.scalar.copy(out=inv_cols[:], in_=banks["w2"][:, 1, 0, :TILES])
+
+        def stage(*jobs):
+            for job in jobs:
+                empty(job)
+                quantise(job)
+
+        nc.gpsimd.memset(inv_rows[:], 0.0)
+        nc.vector.tensor_copy(out=inv_rows[:TILES, :], in_=inv_bf[:])
+
+        unsplit_fp(0)
+        turn(fp_job(0, 0), fp_job(0, 1))
+        stage(fp_job(0, 0), fp_job(0, 1))
+        turn_constants()
+        empty_constants()
         metric_passes(0, 0)
+
+        split_fp(1)
+        turn(fp_job(1, 0), fp_job(1, 1))
+        unsplit_fp(2)
+        turn(fp_job(2, 0), fp_job(2, 1))
+        stage(fp_job(1, 0), fp_job(1, 1))
+        split_fp(3)
+        stage(fp_job(2, 0))
+        split_r(0)
+        stage(fp_job(2, 1))
         metric_passes(1, 0)
 
-        turn(sh_job(0), *r_jobs(0))
+        turn(fp_job(3, 0), fp_job(3, 1), r_job(0, 0), r_job(0, 1))
+        split_sh(0)
+        stage(fp_job(3, 0))
+        split_sh(1)
+        stage(fp_job(3, 1), r_job(0, 0), r_job(0, 1))
+        metric_passes(2, 0)
+
+        turn(sh_job(0), sh_job(1))
+        stage(sh_job(0))
         split_r(1)
-        split_fp(2)
+        stage(sh_job(1))
+        metric_passes(3, 0)
+        for t in range(4):
+            shape_pass(t, 0)
+
+        def step(jobs, behind, units, fillers, unweighed=(), unrounded=()):
+            turn(*jobs)
+            for pair in behind:
+                squash(*pair)
+            for job in jobs:
+                empty(job)
+            todo = list(jobs)
+            for pair in unweighed:
+                weigh(*pair)
+                quantise(todo.pop(0))
+            for pair in unrounded:
+                round_y(*pair)
+                quantise(todo.pop(0))
+            behind = list(behind)
+            for pair in behind:
+                weigh(*pair)
+                if todo:
+                    quantise(todo.pop(0))
+                round_y(*pair)
+            for pair in unweighed:
+                round_y(*pair)
+            for job in todo:
+                quantise(job)
+            fillers = list(fillers)
+            for pair in units[:-1]:
+                unit(*pair)
+                squash(*pair)
+                weigh(*pair)
+                if fillers:
+                    fillers.pop(0)()
+                round_y(*pair)
+            unit(*units[-1])
+
+        turn(r_job(1, 0), r_job(1, 1))
+        squash(0, 0)
+        empty(r_job(1, 0))
+        squash(1, 0)
+        empty(r_job(1, 1))
+        squash(2, 0)
+        squash(3, 0)
+        weigh(0, 0)
+        quantise(r_job(1, 0))
+        round_y(0, 0)
+        split_fp(4)
+        quantise(r_job(1, 1))
+        weigh(1, 0)
         metric_passes(0, 1)
         metric_passes(1, 1)
-        finish(0, 0)
-        finish(1, 0)
-
-        turn(*r_jobs(1), *fp_jobs(2))
+        shape_pass(0, 1)
+        shape_pass(1, 1)
+        unit(2, 1)
+        weigh(2, 0)
+        round_y(1, 0)
         split_r(2)
-        split_sh(1)
-        metric_passes(0, 2)
-        metric_passes(1, 2)
-        finish(0, 1)
-        finish(1, 1)
+        weigh(3, 0)
+        round_y(2, 0)
+        squash(0, 1)
+        squash(1, 1)
+        round_y(3, 0)
+        weigh(0, 1)
 
-        turn(sh_job(1), *r_jobs(2), y_job((0, 0), (1, 0)))
-        split_fp(3)
-        metric_passes(2, 0)
-        metric_passes(2, 1)
-
-        turn(*fp_jobs(3), y_job((0, 1), (1, 1)))
-        split_fp(4)
-        split_sh(2)
-        finish(0, 2)
-        finish(1, 2)
-        finish(2, 0)
-        finish(2, 1)
-        unit(2, 2)
-
-        waiting = [(0, 2), (1, 2)] + [(t, c) for t in range(2, TILES) for c in range(CHUNKS)]
-        stored = 0
-        for t in range(3, TILES):
-            jobs = []
-            if t + 1 < TILES:
-                jobs += fp_jobs(t + 1)
-            if t in (3, 5):
-                jobs.append(sh_job((t + 1) // 2))
-            y_banks = 1 if t in (3, 5) else 2
-            for b in range(y_banks):
-                jobs.append(y_job(*waiting[:2]))
-                waiting = waiting[2:]
-            turn(*jobs)
-            if t + 2 < TILES:
-                split_fp(t + 2)
-            if t == 4:
-                split_sh(3)
-            while stored < waiting[0][0]:
-                store_codes(stored, slice(0, CHUNKS))
-                stored += 1
-            for c in range(CHUNKS):
-                unit(t, c, last=(t == TILES - 1 and c == CHUNKS - 1))
-
-        last = TILES - 1
-        turn(y_job((last - 1, 2), (last, 0)))
-        store_codes(last - 1, slice(0, CHUNKS))
-        store_scales(slice(0, last * P), [nc.sync] * 4)
-        turn(y_job((last, 1)))
-        store_codes(last, slice(0, 2))
-        turn(y_job((last, 2)))
-        store_codes(last, slice(2, 3))
-        store_scales(slice(last * P, M), [nc.scalar, nc.scalar, nc.sync, nc.sync])
+        step(
+            [r_job(2, 0), r_job(2, 1), y_job((0, 0), (1, 0)), y_job((2, 0), (3, 0))],
+            [(2, 1)], [(3, 1), (0, 2), (1, 2)], [lambda: split_sh(2)], [(1, 1)], [(0, 1)]
+        )
+        step(
+            [fp_job(4, 0), fp_job(4, 1), sh_job(2), y_job((0, 1), (1, 1))],
+            [(1, 2)], [(2, 2), (3, 2), (4, 0)], [lambda: split_fp(5)],
+        )
+        step(
+            [fp_job(5, 0), fp_job(5, 1), y_job((2, 1), (3, 1)), y_job((0, 2), (1, 2))],
+            [(4, 0)], [(4, 1), (4, 2), (5, 0)], [lambda: (split_fp(6), split_sh(3))],
+        )
+        store_codes(0, 2)
+        step(
+            [fp_job(6, 0), fp_job(6, 1), sh_job(3), y_job((2, 2), (3, 2))],
+            [(5, 0)], [(5, 1), (5, 2), (6, 0)], [lambda: split_fp(7)],
+        )
+        store_codes(2, 4)
+        step(
+            [fp_job(7, 0), fp_job(7, 1), y_job((4, 0), (4, 1)), y_job((4, 2), (5, 0))],
+            [(6, 0)], [(6, 1), (6, 2)], [],
+        )
+        store_codes(4, 5)
+        step([y_job((5, 1), (5, 2)), y_job((6, 0))], [(6, 2)], [(7, 0), (7, 1)], [])
+        store_codes(5, 6)
+        store_scales(0, 6, [nc.sync] * 4)
+        step([y_job((6, 1), (6, 2))], [(7, 1)], [(7, 2)], [])
+        store_codes(6, 7)
+        turn(y_job((7, 0), (7, 1)))
+        squash(7, 2)
+        empty(y_job((7, 0), (7, 1)))
+        round_y(7, 2, direct=True)
+        weigh(7, 2)
+        quantise(y_job((7, 0), (7, 1)))
+        store_codes(7, 8, slice(0, 2))
+        turn(y_job((7, 2)))
+        stage(y_job((7, 2)))
+        store_codes(7, 8, slice(2, 3))
+        store_scales(6, 8, [nc.scalar, nc.scalar, nc.sync, nc.sync])

@@ -30,7 +30,7 @@ def tile_molecule_metric_scores_g5_kernel(
     with ExitStack() as ctx:
         keep = ctx.enter_context(tc.tile_pool(name="keep", bufs=1))
         work = ctx.enter_context(tc.tile_pool(name="work", bufs=3))
-        psum = ctx.enter_context(tc.psum_pool(name="psum", bufs=4))
+        psum = ctx.enter_context(tc.psum_pool(name="psum", bufs=1))
         ctx.enter_context(tc.manual_schedule())
 
         w_words = keep.tile([P, CHUNKS, 4], BF16)
@@ -40,8 +40,6 @@ def tile_molecule_metric_scores_g5_kernel(
 
         ident = keep.tile([P, P], F32)
         make_identity(nc, ident[:])
-        warm = keep.tile([P, 8], F32)
-        nc.scalar.activation(out=warm[:, 0:1], in_=ident[:, 0:1], func=TANH)
 
         d_words = [keep.tile([P, D_PASSES, 2 * CHUNK], U8, name="d_words%d" % c, align_bytes=256) for c in range(CHUNKS)]
         d_scales = [keep.tile([P, D_PASSES, CHUNK], U8, name="d_scales%d" % c, align_bytes=256) for c in range(CHUNKS)]
@@ -69,14 +67,15 @@ def tile_molecule_metric_scores_g5_kernel(
             nc.sync.dma_start(out=d_words[c][:, first:last, :].bitcast(I32), in_=src.bitcast(I32))
 
         def load_d_scales(c):
-            for q in range(4):
-                rows = metric_scales[:, 4 * q : 4 * q + 4, CHUNK * c : CHUNK * (c + 1)].rearrange("g r n -> r g n")
-                nc.sync.dma_start(out=d_scales[c][32 * q : 32 * q + 4, :, :].bitcast(I32), in_=rows.bitcast(I32))
+            for r in range(4):
+                rows = metric_scales[:, r:16:4, CHUNK * c : CHUNK * (c + 1)].rearrange("g q n -> q g n")
+                nc.sync.dma_start(out=d_scales[c][r:P:32, :, :].bitcast(I32), in_=rows.bitcast(I32))
 
         load_fp(0, 0, 2)
         load_fp(0, 2, 4)
         load_d_scales(0)
-        load_d_words(0)
+        load_d_words(0, 0, 2)
+        load_d_words(0, 2, 4)
         load_fp(1)
         load_fp(2)
         load_fp(3)
@@ -107,6 +106,16 @@ def tile_molecule_metric_scores_g5_kernel(
         w_rows = keep.tile([P, N], BF16)
         inv_rows = keep.tile([P, P], F32)
         inv_cols = keep.tile([P, TILES], F32)
+
+        free_banks = list(range(8))
+        bank_of = {}
+
+        def take_bank(key, shape_):
+            bank_of[key] = free_banks.pop(0)
+            return psum.tile(shape_, F32, tag="bank%d" % bank_of[key], name="bank")
+
+        def give_bank(key):
+            free_banks.append(bank_of[key])
 
         halves = {}
         banks = {}
@@ -156,7 +165,7 @@ def tile_molecule_metric_scores_g5_kernel(
 
         def turn(*jobs):
             for job in jobs:
-                banks[job[0]] = psum.tile([P, 2, 2, P], F32, tag="turn", name="turn")
+                banks[job[0]] = take_bank(job[0], [P, 2, 2, P])
                 for s, key in enumerate(job[0]):
                     for u in range(2):
                         nc.tensor.transpose(banks[job[0]][:, s, u, :], halves[key][u], ident[:])
@@ -169,6 +178,7 @@ def tile_molecule_metric_scores_g5_kernel(
                 out=words.rearrange("p (%s) -> p %s" % (order, order), s=len(keys), u=2),
                 in_=banks[keys][:, : len(keys), :, :].rearrange("p s u r -> p %s" % order),
             )
+            give_bank(keys)
 
         def quantise(job):
             first = 0
@@ -181,7 +191,7 @@ def tile_molecule_metric_scores_g5_kernel(
 
         def metric_passes(t, c, first=0, last=D_PASSES):
             if first == 0:
-                acc[t, c] = psum.tile([P, CHUNK], F32, tag="acc", name="acc")
+                acc[t, c] = take_bank((t, c), [P, CHUNK])
             for g in range(first, last):
                 cols = slice(g * P, (g + 1) * P)
                 nc.tensor.matmul_mx(
@@ -214,6 +224,7 @@ def tile_molecule_metric_scores_g5_kernel(
         def squash(t, c):
             squashed[t, c] = work.tile([P, CHUNK], F32, tag="squashed", name="squashed", bufs=4)
             nc.scalar.activation(out=squashed[t, c][:], in_=acc[t, c][:], func=TANH, scale=inv_cols[:, t : t + 1])
+            give_bank((t, c))
 
         def weigh(t, c):
             cols = slice(c * CHUNK, (c + 1) * CHUNK)
@@ -235,6 +246,30 @@ def tile_molecule_metric_scores_g5_kernel(
                 nc.vector.tensor_copy(out=y_bf[:], in_=y_f32[t, c][:].rearrange(parted, u=2, e=2))
             halves["y", t, c] = [y_bf[:, u, :, :].rearrange("p c e -> p (c e)").bitcast(F32) for u in range(2)]
 
+        def last_unit_quarter(t, c, q):
+            rows = slice(t * P, (t + 1) * P)
+            cols = slice(c * CHUNK + q * P, c * CHUNK + (q + 1) * P)
+            acc[t, c, q] = take_bank((t, c, q), [P, P])
+            for g in range(D_PASSES):
+                nc.tensor.matmul_mx(
+                    out=acc[t, c, q][:],
+                    lhsT=fp_codes[:, t, g * P : (g + 1) * P].bitcast(FP8X4),
+                    lhsT_scale=fp_scales[:, t, g * P : (g + 1) * P],
+                    rhs=d_words[c][:, g, 2 * P * q : 2 * P * (q + 1)].bitcast(FP4X4),
+                    rhs_scale=d_scales[c][:, g, P * q : P * (q + 1)],
+                    start=(g == 0),
+                    stop=False,
+                )
+            nc.tensor.matmul_mx(
+                out=acc[t, c, q][:],
+                lhsT=sh_codes[:, rows].bitcast(FP8X4),
+                lhsT_scale=sh_scales[:, rows],
+                rhs=r_codes[:, cols].bitcast(FP8X4),
+                rhs_scale=r_scales[:, cols],
+                start=False,
+                stop=True,
+            )
+
         code_rows = out_1.rearrange("g p m t -> p g (m t)")
 
         def store_codes(first, last, groups=slice(0, CHUNKS)):
@@ -243,17 +278,16 @@ def tile_molecule_metric_scores_g5_kernel(
                 in_=y_codes[:, groups, first * P : last * P].bitcast(I32),
             )
 
-        def store_scales(first, last, queues):
-            cols = slice(first * P, last * P)
-            for q in range(4):
-                queues[q].dma_start(
-                    out=out_2[:, 4 * q : 4 * q + 4, cols].rearrange("g r m -> r g m").bitcast(I32),
-                    in_=y_scales[32 * q : 32 * q + 4, :, cols].bitcast(I32),
+        def store_scales(groups, queues):
+            for r in range(4):
+                queues[r].dma_start(
+                    out=out_2[groups, r:16:4, :].rearrange("g q m -> q g m").bitcast(I32),
+                    in_=y_scales[r:P:32, groups, :].bitcast(I32),
                 )
 
         def turn_constants():
             for key, chunks in (("w01", (0, 1)), ("w2", (2,))):
-                banks[key] = psum.tile([P, 2, 2, P], F32, tag="turn", name="turn")
+                banks[key] = take_bank(key, [P, 2, 2, P])
                 for s, c in enumerate(chunks):
                     for u in range(2):
                         column = w_words[:, c, :].bitcast(F32)[:, u : u + 1]
@@ -265,6 +299,8 @@ def tile_molecule_metric_scores_g5_kernel(
             nc.scalar.copy(out=w_out[:, :2, :, :], in_=banks["w01"][:].rearrange("p s u r -> p s r u"))
             nc.scalar.copy(out=w_out[:, 2, :, :], in_=banks["w2"][:, 0, :, :].rearrange("p u r -> p r u"))
             nc.scalar.copy(out=inv_cols[:], in_=banks["w2"][:, 1, 0, :TILES])
+            give_bank("w01")
+            give_bank("w2")
 
         def stage(*jobs):
             for job in jobs:
@@ -292,118 +328,124 @@ def tile_molecule_metric_scores_g5_kernel(
         stage(fp_job(2, 1))
         metric_passes(1, 0)
 
-        turn(fp_job(3, 0), fp_job(3, 1), r_job(0, 0), r_job(0, 1))
         split_sh(0)
-        stage(fp_job(3, 0))
         split_sh(1)
-        stage(fp_job(3, 1), r_job(0, 0), r_job(0, 1))
-        metric_passes(2, 0)
-
-        turn(sh_job(0), sh_job(1))
-        stage(sh_job(0))
+        turn(fp_job(3, 0), fp_job(3, 1), r_job(0, 0), r_job(0, 1), sh_job(0), sh_job(1))
+        stage(fp_job(3, 0), fp_job(3, 1), r_job(0, 0), r_job(0, 1), sh_job(0))
         split_r(1)
         stage(sh_job(1))
+        metric_passes(2, 0)
         metric_passes(3, 0)
         for t in range(4):
             shape_pass(t, 0)
 
-        def step(jobs, behind, units, fillers, unweighed=(), unrounded=()):
+
+        unrounded = []
+
+        def weigh_next(pair):
+            weigh(*pair)
+            while unrounded:
+                round_y(*unrounded.pop(0))
+            unrounded.append(pair)
+
+        def step(jobs, behind, units, splits=(), stores=()):
             turn(*jobs)
-            for pair in behind:
-                squash(*pair)
+            squash(*behind)
             for job in jobs:
                 empty(job)
-            todo = list(jobs)
-            for pair in unweighed:
-                weigh(*pair)
-                quantise(todo.pop(0))
-            for pair in unrounded:
-                round_y(*pair)
-                quantise(todo.pop(0))
-            behind = list(behind)
-            for pair in behind:
-                weigh(*pair)
-                if todo:
-                    quantise(todo.pop(0))
-                round_y(*pair)
-            for pair in unweighed:
-                round_y(*pair)
-            for job in todo:
+            weigh_next(behind)
+            operands = [job for job in jobs if job[0][0][0] != "y"]
+            results = [job for job in jobs if job[0][0][0] == "y"]
+            for job in operands:
                 quantise(job)
-            fillers = list(fillers)
-            for pair in units[:-1]:
+            for do_split, index in splits:
+                do_split(index)
+            for number, pair in enumerate(units[:-1]):
                 unit(*pair)
                 squash(*pair)
-                weigh(*pair)
-                if fillers:
-                    fillers.pop(0)()
-                round_y(*pair)
+                if number == 0:
+                    for job in results:
+                        quantise(job)
+                    for store in stores:
+                        store()
+                    round_y(*unrounded.pop(0))
+                weigh_next(pair)
+            round_y(*unrounded.pop(0))
             unit(*units[-1])
 
         turn(r_job(1, 0), r_job(1, 1))
         squash(0, 0)
-        empty(r_job(1, 0))
         squash(1, 0)
+        empty(r_job(1, 0))
         empty(r_job(1, 1))
         squash(2, 0)
         squash(3, 0)
-        weigh(0, 0)
+        weigh_next((0, 0))
+        weigh_next((1, 0))
         quantise(r_job(1, 0))
-        round_y(0, 0)
-        split_fp(4)
         quantise(r_job(1, 1))
-        weigh(1, 0)
         metric_passes(0, 1)
         metric_passes(1, 1)
         shape_pass(0, 1)
         shape_pass(1, 1)
         unit(2, 1)
-        weigh(2, 0)
-        round_y(1, 0)
         split_r(2)
-        weigh(3, 0)
-        round_y(2, 0)
+        split_fp(4)
+        weigh_next((2, 0))
+        weigh_next((3, 0))
         squash(0, 1)
         squash(1, 1)
-        round_y(3, 0)
-        weigh(0, 1)
+        weigh_next((0, 1))
+        weigh_next((1, 1))
 
         step(
-            [r_job(2, 0), r_job(2, 1), y_job((0, 0), (1, 0)), y_job((2, 0), (3, 0))],
-            [(2, 1)], [(3, 1), (0, 2), (1, 2)], [lambda: split_sh(2)], [(1, 1)], [(0, 1)]
+            [r_job(2, 0), r_job(2, 1), fp_job(4, 0), fp_job(4, 1), y_job((0, 0), (1, 0))],
+            (2, 1), [(3, 1), (0, 2), (1, 2), (2, 2)], [(split_sh, 2), (split_fp, 5)],
         )
         step(
-            [fp_job(4, 0), fp_job(4, 1), sh_job(2), y_job((0, 1), (1, 1))],
-            [(1, 2)], [(2, 2), (3, 2), (4, 0)], [lambda: split_fp(5)],
+            [sh_job(2), fp_job(5, 0), fp_job(5, 1), y_job((2, 0), (3, 0)), y_job((0, 1), (1, 1))],
+            (2, 2), [(3, 2), (4, 0), (4, 1)], [(split_fp, 6), (split_sh, 3)],
+            [lambda: store_codes(0, 4, slice(0, 1))],
         )
         step(
-            [fp_job(5, 0), fp_job(5, 1), y_job((2, 1), (3, 1)), y_job((0, 2), (1, 2))],
-            [(4, 0)], [(4, 1), (4, 2), (5, 0)], [lambda: (split_fp(6), split_sh(3))],
+            [fp_job(6, 0), fp_job(6, 1), sh_job(3), y_job((2, 1), (3, 1)), y_job((0, 2), (1, 2))],
+            (4, 1), [(5, 0), (5, 1)], [(split_fp, 7)],
+            [lambda: store_codes(0, 4, slice(1, 2))],
         )
-        store_codes(0, 2)
         step(
-            [fp_job(6, 0), fp_job(6, 1), sh_job(3), y_job((2, 2), (3, 2))],
-            [(5, 0)], [(5, 1), (5, 2), (6, 0)], [lambda: split_fp(7)],
+            [fp_job(7, 0), fp_job(7, 1), y_job((2, 2), (3, 2)), y_job((4, 0), (5, 0))],
+            (5, 1), [(6, 0), (6, 1), (7, 0), (7, 1), (4, 2)], [],
+            [lambda: store_codes(0, 4, slice(2, 3))],
         )
-        store_codes(2, 4)
         step(
-            [fp_job(7, 0), fp_job(7, 1), y_job((4, 0), (4, 1)), y_job((4, 2), (5, 0))],
-            [(6, 0)], [(6, 1), (6, 2)], [],
+            [y_job((4, 1), (5, 1)), y_job((6, 0), (7, 0)), y_job((6, 1), (7, 1))],
+            (4, 2), [(5, 2), (6, 2)], [],
+            [lambda: store_codes(4, 8, slice(0, 2)), lambda: store_scales(slice(0, 2), [nc.sync] * 4)],
         )
-        store_codes(4, 5)
-        step([y_job((5, 1), (5, 2)), y_job((6, 0))], [(6, 2)], [(7, 0), (7, 1)], [])
-        store_codes(5, 6)
-        store_scales(0, 6, [nc.sync] * 4)
-        step([y_job((6, 1), (6, 2))], [(7, 1)], [(7, 2)], [])
-        store_codes(6, 7)
-        turn(y_job((7, 0), (7, 1)))
-        squash(7, 2)
-        empty(y_job((7, 0), (7, 1)))
-        round_y(7, 2, direct=True)
-        weigh(7, 2)
-        quantise(y_job((7, 0), (7, 1)))
-        store_codes(7, 8, slice(0, 2))
-        turn(y_job((7, 2)))
-        stage(y_job((7, 2)))
-        store_codes(7, 8, slice(2, 3))
-        store_scales(6, 8, [nc.scalar, nc.scalar, nc.sync, nc.sync])
+        t, c = TILES - 1, CHUNKS - 1
+        squash(t - 1, c)
+        weigh(t - 1, c)
+        squashed[t, c] = work.tile([P, CHUNK], F32, tag="squashed", name="squashed", bufs=4)
+        y_last = work.tile([P, 2, P, 2], BF16, tag="y_bf", bufs=10)
+        halves["y", t, c] = [y_last[:, u, :, :].rearrange("p c e -> p (c e)").bitcast(F32) for u in range(2)]
+        for q in range(4):
+            last_unit_quarter(t, c, q)
+            part = squashed[t, c][:, q * P : (q + 1) * P]
+            nc.scalar.activation(out=part, in_=acc[t, c, q][:], func=TANH, scale=inv_cols[:, t : t + 1])
+            give_bank((t, c, q))
+            nc.vector.tensor_tensor(
+                out=y_last[:, :, 32 * q : 32 * (q + 1), :],
+                in0=part.rearrange("p (c u e) -> p u c e", u=2, e=2),
+                in1=w_rows[:, c * CHUNK + q * P : c * CHUNK + (q + 1) * P].rearrange("p (c u e) -> p u c e", u=2, e=2),
+                op=MULT,
+            )
+            if q == 1:
+                round_y(t - 1, c)
+        early, mid, late = y_job((t - 3, c), (t - 2, c)), y_job((t - 1, c)), y_job((t, c))
+        turn(early, mid, late)
+        weigh(t, c)
+        stage(early, mid)
+        store_codes(t - 3, t, slice(2, 3))
+        stage(late)
+        store_codes(t, t + 1, slice(2, 3))
+        store_scales(slice(2, 3), [nc.scalar, nc.scalar, nc.sync, nc.sync])

@@ -38,11 +38,16 @@ def tile_molecule_metric_scores_g5_kernel(
         inv_bf = keep.tile([TILES, P], BF16)
         nc.scalar.dma_start(out=inv_bf[:], in_=inv_size.rearrange("(t p) -> t p", p=P))
 
+        zeros = keep.tile([P, 8 * P], BF16, align_bytes=256)
+        nc.gpsimd.memset(zeros[:].bitcast(I32), 0)
         ident = keep.tile([P, P], F32)
         make_identity(nc, ident[:])
 
         d_words = [keep.tile([P, D_PASSES, 2 * CHUNK], U8, name="d_words%d" % c, align_bytes=256) for c in range(CHUNKS)]
         d_scales = [keep.tile([P, D_PASSES, CHUNK], U8, name="d_scales%d" % c, align_bytes=256) for c in range(CHUNKS)]
+        warm_codes = keep.tile([P, 2 * P], U32, align_bytes=256)
+        warm_scales = keep.tile([P, 2 * P], U8, align_bytes=256)
+        nc.vector.quantize_mx(out=warm_codes[:].bitcast(FP8X4), scales=warm_scales[:], in_=zeros[:])
         for c in range(CHUNKS):
             nc.vector.memset(d_scales[c][:].bitcast(I32), 0)
 
@@ -75,8 +80,8 @@ def tile_molecule_metric_scores_g5_kernel(
         load_fp(0, 2, 4)
         load_d_scales(0)
         load_d_words(0, 0, 2)
-        load_d_words(0, 2, 4)
         load_fp(1)
+        load_d_words(0, 2, 4)
         load_fp(2)
         load_fp(3)
         load_sh(0)
@@ -310,35 +315,52 @@ def tile_molecule_metric_scores_g5_kernel(
         nc.gpsimd.memset(inv_rows[:], 0.0)
         nc.vector.tensor_copy(out=inv_rows[:TILES, :], in_=inv_bf[:])
 
+        warm_bank = take_bank("warm", [P, 2 * P])
+        for repeat in range(7):
+            nc.tensor.matmul_mx(
+                out=warm_bank[:],
+                lhsT=warm_codes[:, :P].bitcast(FP8X4),
+                lhsT_scale=warm_scales[:, :P],
+                rhs=warm_codes[:].bitcast(FP8X4),
+                rhs_scale=warm_scales[:],
+                start=True,
+                stop=True,
+            )
+        give_bank("warm")
+
         unsplit_fp(0)
         turn(fp_job(0, 0), fp_job(0, 1))
         stage(fp_job(0, 0), fp_job(0, 1))
         turn_constants()
         empty_constants()
-        metric_passes(0, 0)
+        metric_passes(0, 0, 0, 2)
 
-        split_fp(1)
+        unsplit_fp(1)
         turn(fp_job(1, 0), fp_job(1, 1))
+        stage(fp_job(1, 0), fp_job(1, 1))
+        metric_passes(0, 0, 2, 4)
+
         unsplit_fp(2)
         turn(fp_job(2, 0), fp_job(2, 1))
-        stage(fp_job(1, 0), fp_job(1, 1))
         split_fp(3)
         stage(fp_job(2, 0))
-        split_r(0)
+        split_sh(0)
         stage(fp_job(2, 1))
         metric_passes(1, 0)
 
-        split_sh(0)
+        turn(fp_job(3, 0), fp_job(3, 1), sh_job(0))
+        split_r(0)
         split_sh(1)
-        turn(fp_job(3, 0), fp_job(3, 1), r_job(0, 0), r_job(0, 1), sh_job(0), sh_job(1))
-        stage(fp_job(3, 0), fp_job(3, 1), r_job(0, 0), r_job(0, 1), sh_job(0))
-        split_r(1)
-        stage(sh_job(1))
+        stage(fp_job(3, 0), fp_job(3, 1), sh_job(0))
         metric_passes(2, 0)
+
+        turn(r_job(0, 0), r_job(0, 1), sh_job(1))
+        stage(r_job(0, 0), r_job(0, 1), sh_job(1))
+        split_r(1)
         metric_passes(3, 0)
+        metric_passes(0, 1)
         for t in range(4):
             shape_pass(t, 0)
-
 
         unrounded = []
 
@@ -350,12 +372,16 @@ def tile_molecule_metric_scores_g5_kernel(
 
         def step(jobs, behind, units, splits=(), stores=()):
             turn(*jobs)
-            squash(*behind)
+            for pair in behind:
+                squash(*pair)
             for job in jobs:
                 empty(job)
-            weigh_next(behind)
             operands = [job for job in jobs if job[0][0][0] != "y"]
             results = [job for job in jobs if job[0][0][0] == "y"]
+            for pair in behind:
+                weigh_next(pair)
+                if operands:
+                    quantise(operands.pop(0))
             for job in operands:
                 quantise(job)
             for do_split, index in splits:
@@ -384,42 +410,38 @@ def tile_molecule_metric_scores_g5_kernel(
         weigh_next((1, 0))
         quantise(r_job(1, 0))
         quantise(r_job(1, 1))
-        metric_passes(0, 1)
         metric_passes(1, 1)
+        metric_passes(2, 1)
         shape_pass(0, 1)
         shape_pass(1, 1)
-        unit(2, 1)
+        shape_pass(2, 1)
         split_r(2)
         split_fp(4)
         weigh_next((2, 0))
         weigh_next((3, 0))
-        squash(0, 1)
-        squash(1, 1)
-        weigh_next((0, 1))
-        weigh_next((1, 1))
 
         step(
             [r_job(2, 0), r_job(2, 1), fp_job(4, 0), fp_job(4, 1), y_job((0, 0), (1, 0))],
-            (2, 1), [(3, 1), (0, 2), (1, 2), (2, 2)], [(split_sh, 2), (split_fp, 5)],
+            [(0, 1), (1, 1), (2, 1)], [(3, 1), (0, 2), (1, 2), (2, 2)], [(split_sh, 2), (split_fp, 5)],
         )
         step(
             [sh_job(2), fp_job(5, 0), fp_job(5, 1), y_job((2, 0), (3, 0)), y_job((0, 1), (1, 1))],
-            (2, 2), [(3, 2), (4, 0), (4, 1)], [(split_fp, 6), (split_sh, 3)],
+            [(2, 2)], [(3, 2), (4, 0), (4, 1)], [(split_fp, 6), (split_sh, 3)],
             [lambda: store_codes(0, 4, slice(0, 1))],
         )
         step(
             [fp_job(6, 0), fp_job(6, 1), sh_job(3), y_job((2, 1), (3, 1)), y_job((0, 2), (1, 2))],
-            (4, 1), [(5, 0), (5, 1)], [(split_fp, 7)],
+            [(4, 1)], [(5, 0), (5, 1)], [(split_fp, 7)],
             [lambda: store_codes(0, 4, slice(1, 2))],
         )
         step(
-            [fp_job(7, 0), fp_job(7, 1), y_job((2, 2), (3, 2)), y_job((4, 0), (5, 0))],
-            (5, 1), [(6, 0), (6, 1), (7, 0), (7, 1), (4, 2)], [],
+            [fp_job(7, 0), fp_job(7, 1), y_job((2, 2), (3, 2)), y_job((4, 0), (4, 1))],
+            [(5, 1)], [(6, 0), (6, 1), (7, 0), (7, 1), (4, 2)], [],
             [lambda: store_codes(0, 4, slice(2, 3))],
         )
         step(
-            [y_job((4, 1), (5, 1)), y_job((6, 0), (7, 0)), y_job((6, 1), (7, 1))],
-            (4, 2), [(5, 2), (6, 2)], [],
+            [y_job((5, 0), (5, 1)), y_job((6, 0), (7, 0)), y_job((6, 1), (7, 1))],
+            [(4, 2)], [(5, 2), (6, 2)], [],
             [lambda: store_codes(4, 8, slice(0, 2)), lambda: store_scales(slice(0, 2), [nc.sync] * 4)],
         )
         t, c = TILES - 1, CHUNKS - 1

from contextlib import ExitStack

import concourse.mybir as mybir
from concourse.masks import make_identity

M, N, E, K = 1024, 1536, 512, 2048
FLOPS = 2 * M * N * (E + K)

F32 = mybir.dt.float32
BF16 = mybir.dt.bfloat16
I32 = mybir.dt.int32
U32 = mybir.dt.uint32
U8 = mybir.dt.uint8
FP8X4 = mybir.dt.float8_e4m3fn_x4
FP4X4 = mybir.dt.float4_e2m1fn_x4
TANH = mybir.ActivationFunctionType.Tanh
MULT = mybir.AluOpType.mult

P = 128
CHUNK = 512
TILES = M // P
CHUNKS = N // CHUNK
D_PASSES = K // 512


def tile_molecule_metric_scores_g5_kernel(
    tc, fingerprint, shape, ref_shape, metric_words, metric_scales, inv_size, ref_weight, out_0, out_1, out_2
):
    nc = tc.nc
    with ExitStack() as ctx:
        keep = ctx.enter_context(tc.tile_pool(name="keep", bufs=1))
        work = ctx.enter_context(tc.tile_pool(name="work", bufs=3))
        psum = ctx.enter_context(tc.psum_pool(name="psum", bufs=1))
        ctx.enter_context(tc.manual_schedule())

        w_words = keep.tile([P, CHUNKS, 4], BF16)
        nc.scalar.dma_start(out=w_words[:], in_=ref_weight.rearrange("(c p t) -> p c t", p=P, t=4))
        inv_bf = keep.tile([TILES, P], BF16)
        nc.scalar.dma_start(out=inv_bf[:], in_=inv_size.rearrange("(t p) -> t p", p=P))

        zeros = keep.tile([P, 8 * P], BF16, align_bytes=256)
        nc.gpsimd.memset(zeros[:].bitcast(I32), 0)
        ident = keep.tile([P, P], F32)
        make_identity(nc, ident[:])

        d_words = [keep.tile([P, D_PASSES, 2 * CHUNK], U8, name="d_words%d" % c, align_bytes=256) for c in range(CHUNKS)]
        d_scales = [keep.tile([P, D_PASSES, CHUNK], U8, name="d_scales%d" % c, align_bytes=256) for c in range(CHUNKS)]
        warm_codes = keep.tile([P, 2 * P], U32, align_bytes=256)
        warm_scales = keep.tile([P, 2 * P], U8, align_bytes=256)
        nc.vector.quantize_mx(out=warm_codes[:].bitcast(FP8X4), scales=warm_scales[:], in_=zeros[:])
        for c in range(CHUNKS):
            nc.vector.memset(d_scales[c][:].bitcast(I32), 0)

        fp_raw = [keep.tile([P, K], BF16, name="fp_raw%d" % t) for t in range(TILES)]
        sh_raw = [keep.tile([P, 2 * E], BF16, name="sh_raw%d" % h) for h in range(TILES // 2)]
        r_raw = [keep.tile([P, 2, 2 * E], BF16, name="r_raw%d" % c) for c in range(CHUNKS)]

        def load_fp(t, first=0, last=D_PASSES):
            cols = slice(512 * first, 512 * last)
            nc.sync.dma_start(out=fp_raw[t][:, cols], in_=fingerprint[t * P : (t + 1) * P, cols])

        def load_sh(h):
            rows = shape[2 * P * h : 2 * P * (h + 1), :]
            nc.sync.dma_start(out=sh_raw[h][:], in_=rows.rearrange("(r b) k -> r (b k)", b=2))

        def load_r(c):
            rows = ref_shape[CHUNK * c : CHUNK * (c + 1), :]
            nc.sync.dma_start(out=r_raw[c][:], in_=rows.rearrange("(h r b) k -> r h (b k)", h=2, b=2))

        def load_d_words(c, first=0, last=D_PASSES):
            src = metric_words[first:last, :, 2 * CHUNK * c : 2 * CHUNK * (c + 1)].rearrange("g p b -> p g b")
            nc.sync.dma_start(out=d_words[c][:, first:last, :].bitcast(I32), in_=src.bitcast(I32))

        def load_d_scales(c):
            for r in range(4):
                rows = metric_scales[:, r:16:4, CHUNK * c : CHUNK * (c + 1)].rearrange("g q n -> q g n")
                nc.sync.dma_start(out=d_scales[c][r:P:32, :, :].bitcast(I32), in_=rows.bitcast(I32))

        load_fp(0, 0, 2)
        load_fp(0, 2, 4)
        load_d_scales(0)
        load_d_words(0, 0, 2)
        load_fp(1)
        load_d_words(0, 2, 4)
        load_fp(2)
        load_fp(3)
        load_sh(0)
        load_r(0)
        load_sh(1)
        load_d_words(1)
        load_d_scales(1)
        load_r(1)
        load_d_words(2)
        load_d_scales(2)
        load_r(2)
        load_fp(4)
        load_sh(2)
        load_fp(5)
        load_fp(6)
        load_sh(3)
        load_fp(7)

        fp_codes = keep.tile([P, TILES, D_PASSES * P], U32, align_bytes=256)
        fp_scales = keep.tile([P, TILES, D_PASSES * P], U8, align_bytes=256)
        sh_codes = keep.tile([P, M], U32, align_bytes=256)
        sh_scales = keep.tile([P, M], U8, align_bytes=256)
        r_codes = keep.tile([P, N], U32, align_bytes=256)
        r_scales = keep.tile([P, N], U8, align_bytes=256)
        y_codes = keep.tile([P, CHUNKS, M], U32, align_bytes=256)
        y_scales = keep.tile([P, CHUNKS, M], U8, align_bytes=256)
        w_rows = keep.tile([P, N], BF16)
        inv_rows = keep.tile([P, P], F32)
        inv_cols = keep.tile([P, TILES], F32)

        free_banks = list(range(8))
        bank_of = {}

        def take_bank(key, shape_):
            bank_of[key] = free_banks.pop(0)
            return psum.tile(shape_, F32, tag="bank%d" % bank_of[key], name="bank")

        def give_bank(key):
            free_banks.append(bank_of[key])

        halves = {}
        banks = {}
        staged = {}
        acc = {}
        squashed = {}
        y_f32 = {}

        def split(key, raw, count):
            parted = work.tile([P, count, 2, P], F32, tag="parted%d" % count, name="parted")
            nc.vector.tensor_copy(out=parted[:], in_=raw.bitcast(F32).rearrange("p (s c u) -> p s u c", u=2, c=P))
            for s in range(count):
                halves[key + (s,)] = [parted[:, s, u, :] for u in range(2)]

        def split_fp(t):
            split(("fp", t), fp_raw[t][:], D_PASSES)

        def split_sh(h):
            split(("sh", h), sh_raw[h][:], 2)

        def split_r(c):
            split(("r", c), r_raw[c][:].rearrange("p h k -> p (h k)"), 4)

        def unsplit_fp(t):
            words = fp_raw[t][:].bitcast(F32)
            for g in range(D_PASSES):
                halves["fp", t, g] = [words[:, 2 * P * g + u : 2 * P * (g + 1) : 2] for u in range(2)]

        def fp_job(t, a):
            cols = slice(2 * a * P, 2 * (a + 1) * P)
            return (("fp", t, 2 * a), ("fp", t, 2 * a + 1)), "s r u", [(fp_codes[:, t, cols], fp_scales[:, t, cols])]

        def sh_job(h):
            cols = slice(2 * P * h, 2 * P * (h + 1))
            return (("sh", h, 0), ("sh", h, 1)), "r s u", [(sh_codes[:, cols], sh_scales[:, cols])]

        def r_job(c, a):
            cols = slice(CHUNK * c + 2 * P * a, CHUNK * c + 2 * P * (a + 1))
            return (("r", c, 2 * a), ("r", c, 2 * a + 1)), "r s u", [(r_codes[:, cols], r_scales[:, cols])]

        def y_job(*units):
            spans = [(c, t, t + 1) for t, c in units]
            if len(units) == 2 and units[1] == (units[0][0] + 1, units[0][1]):
                spans = [(units[0][1], units[0][0], units[0][0] + 2)]
            targets = [(y_codes[:, c, a * P : b * P], y_scales[:, c, a * P : b * P]) for c, a, b in spans]
            return tuple(("y",) + pair for pair in units), "s r u", targets

        def turn(*jobs):
            for job in jobs:
                banks[job[0]] = take_bank(job[0], [P, 2, 2, P])
                for s, key in enumerate(job[0]):
                    for u in range(2):
                        nc.tensor.transpose(banks[job[0]][:, s, u, :], halves[key][u], ident[:])

        def empty(job):
            keys, order = job[0], job[1]
            staged[keys] = work.tile([P, 2 * 4 * P], BF16, tag="staged", name="staged", bufs=6, align_bytes=64)
            words = staged[keys][:, : len(keys) * 4 * P].bitcast(F32)
            nc.scalar.copy(
                out=words.rearrange("p (%s) -> p %s" % (order, order), s=len(keys), u=2),
                in_=banks[keys][:, : len(keys), :, :].rearrange("p s u r -> p %s" % order),
            )
            give_bank(keys)

        def quantise(job):
            first = 0
            for codes, scales in job[2]:
                width = 4 * codes.shape[1]
                nc.vector.quantize_mx(
                    out=codes.bitcast(FP8X4), scales=scales, in_=staged[job[0]][:, first : first + width]
                )
                first += width

        def metric_passes(t, c, first=0, last=D_PASSES):
            if first == 0:
                acc[t, c] = take_bank((t, c), [P, CHUNK])
            for g in range(first, last):
                cols = slice(g * P, (g + 1) * P)
                nc.tensor.matmul_mx(
                    out=acc[t, c][:],
                    lhsT=fp_codes[:, t, cols].bitcast(FP8X4),
                    lhsT_scale=fp_scales[:, t, cols],
                    rhs=d_words[c][:, g, :].bitcast(FP4X4),
                    rhs_scale=d_scales[c][:, g, :],
                    start=(g == 0),
                    stop=False,
                )

        def shape_pass(t, c):
            rows = slice(t * P, (t + 1) * P)
            cols = slice(c * CHUNK, (c + 1) * CHUNK)
            nc.tensor.matmul_mx(
                out=acc[t, c][:],
                lhsT=sh_codes[:, rows].bitcast(FP8X4),
                lhsT_scale=sh_scales[:, rows],
                rhs=r_codes[:, cols].bitcast(FP8X4),
                rhs_scale=r_scales[:, cols],
                start=False,
                stop=True,
            )

        def unit(t, c):
            metric_passes(t, c)
            shape_pass(t, c)

        def squash(t, c):
            squashed[t, c] = work.tile([P, CHUNK], F32, tag="squashed", name="squashed", bufs=4)
            nc.scalar.activation(out=squashed[t, c][:], in_=acc[t, c][:], func=TANH, scale=inv_cols[:, t : t + 1])
            give_bank((t, c))

        def weigh(t, c):
            cols = slice(c * CHUNK, (c + 1) * CHUNK)
            y_f32[t, c] = work.tile([P, CHUNK], F32, tag="y", name="y", bufs=12)
            nc.vector.tensor_tensor(out=y_f32[t, c][:], in0=squashed[t, c][:], in1=w_rows[:, cols], op=MULT)
            nc.sync.dma_start(out=out_0[t * P : (t + 1) * P, cols], in_=y_f32[t, c][:])

        def round_y(t, c, direct=False):
            y_bf = work.tile([P, 2, P, 2], BF16, tag="y_bf", bufs=10)
            parted = "p (c u e) -> p u c e"
            if direct:
                nc.vector.tensor_tensor(
                    out=y_bf[:],
                    in0=squashed[t, c][:].rearrange(parted, u=2, e=2),
                    in1=w_rows[:, c * CHUNK : (c + 1) * CHUNK].rearrange(parted, u=2, e=2),
                    op=MULT,
                )
            else:
                nc.vector.tensor_copy(out=y_bf[:], in_=y_f32[t, c][:].rearrange(parted, u=2, e=2))
            halves["y", t, c] = [y_bf[:, u, :, :].rearrange("p c e -> p (c e)").bitcast(F32) for u in range(2)]

        def last_unit_quarter(t, c, q):
            rows = slice(t * P, (t + 1) * P)
            cols = slice(c * CHUNK + q * P, c * CHUNK + (q + 1) * P)
            acc[t, c, q] = take_bank((t, c, q), [P, P])
            for g in range(D_PASSES):
                nc.tensor.matmul_mx(
                    out=acc[t, c, q][:],
                    lhsT=fp_codes[:, t, g * P : (g + 1) * P].bitcast(FP8X4),
                    lhsT_scale=fp_scales[:, t, g * P : (g + 1) * P],
                    rhs=d_words[c][:, g, 2 * P * q : 2 * P * (q + 1)].bitcast(FP4X4),
                    rhs_scale=d_scales[c][:, g, P * q : P * (q + 1)],
                    start=(g == 0),
                    stop=False,
                )
            nc.tensor.matmul_mx(
                out=acc[t, c, q][:],
                lhsT=sh_codes[:, rows].bitcast(FP8X4),
                lhsT_scale=sh_scales[:, rows],
                rhs=r_codes[:, cols].bitcast(FP8X4),
                rhs_scale=r_scales[:, cols],
                start=False,
                stop=True,
            )

        code_rows = out_1.rearrange("g p m t -> p g (m t)")

        def store_codes(first, last, groups=slice(0, CHUNKS)):
            nc.sync.dma_start(
                out=code_rows[:, groups, 4 * P * first : 4 * P * last].bitcast(I32),
                in_=y_codes[:, groups, first * P : last * P].bitcast(I32),
            )

        def store_scales(groups, queues):
            for r in range(4):
                queues[r].dma_start(
                    out=out_2[groups, r:16:4, :].rearrange("g q m -> q g m").bitcast(I32),
                    in_=y_scales[r:P:32, groups, :].bitcast(I32),
                )

        def turn_constants():
            for key, chunks in (("w01", (0, 1)), ("w2", (2,))):
                banks[key] = take_bank(key, [P, 2, 2, P])
                for s, c in enumerate(chunks):
                    for u in range(2):
                        column = w_words[:, c, :].bitcast(F32)[:, u : u + 1]
                        nc.tensor.transpose(banks[key][:, s, u, :], column.to_broadcast([P, P]), ident[:])
            nc.tensor.transpose(banks["w2"][:, 1, 0, :], inv_rows[:], ident[:])

        def empty_constants():
            w_out = w_rows[:].bitcast(F32).rearrange("p (c r u) -> p c r u", c=CHUNKS, u=2)
            nc.scalar.copy(out=w_out[:, :2, :, :], in_=banks["w01"][:].rearrange("p s u r -> p s r u"))
            nc.scalar.copy(out=w_out[:, 2, :, :], in_=banks["w2"][:, 0, :, :].rearrange("p u r -> p r u"))
            nc.scalar.copy(out=inv_cols[:], in_=banks["w2"][:, 1, 0, :TILES])
            give_bank("w01")
            give_bank("w2")

        def stage(*jobs):
            for job in jobs:
                empty(job)
                quantise(job)

        nc.gpsimd.memset(inv_rows[:], 0.0)
        nc.vector.tensor_copy(out=inv_rows[:TILES, :], in_=inv_bf[:])

        warm_bank = take_bank("warm", [P, 2 * P])
        for repeat in range(7):
            nc.tensor.matmul_mx(
                out=warm_bank[:],
                lhsT=warm_codes[:, :P].bitcast(FP8X4),
                lhsT_scale=warm_scales[:, :P],
                rhs=warm_codes[:].bitcast(FP8X4),
                rhs_scale=warm_scales[:],
                start=True,
                stop=True,
            )
        give_bank("warm")

        unsplit_fp(0)
        turn(fp_job(0, 0), fp_job(0, 1))
        stage(fp_job(0, 0), fp_job(0, 1))
        turn_constants()
        empty_constants()
        metric_passes(0, 0, 0, 2)

        unsplit_fp(1)
        turn(fp_job(1, 0), fp_job(1, 1))
        stage(fp_job(1, 0), fp_job(1, 1))
        metric_passes(0, 0, 2, 4)

        unsplit_fp(2)
        turn(fp_job(2, 0), fp_job(2, 1))
        split_fp(3)
        stage(fp_job(2, 0))
        split_sh(0)
        stage(fp_job(2, 1))
        metric_passes(1, 0)

        turn(fp_job(3, 0), fp_job(3, 1), sh_job(0))
        split_r(0)
        split_sh(1)
        stage(fp_job(3, 0), fp_job(3, 1), sh_job(0))
        metric_passes(2, 0)

        turn(r_job(0, 0), r_job(0, 1), sh_job(1))
        stage(r_job(0, 0), r_job(0, 1), sh_job(1))
        split_r(1)
        metric_passes(3, 0)
        metric_passes(0, 1)
        for t in range(4):
            shape_pass(t, 0)

        unrounded = []

        def weigh_next(pair):
            weigh(*pair)
            while unrounded:
                round_y(*unrounded.pop(0))
            unrounded.append(pair)

        def step(jobs, behind, units, splits=(), stores=()):
            turn(*jobs)
            for pair in behind:
                squash(*pair)
            for job in jobs:
                empty(job)
            operands = [job for job in jobs if job[0][0][0] != "y"]
            results = [job for job in jobs if job[0][0][0] == "y"]
            for pair in behind:
                weigh_next(pair)
                if operands:
                    quantise(operands.pop(0))
            for job in operands:
                quantise(job)
            for do_split, index in splits:
                do_split(index)
            for number, pair in enumerate(units[:-1]):
                unit(*pair)
                squash(*pair)
                if number == 0:
                    for job in results:
                        quantise(job)
                    for store in stores:
                        store()
                    round_y(*unrounded.pop(0))
                weigh_next(pair)
            round_y(*unrounded.pop(0))
            unit(*units[-1])

        turn(r_job(1, 0), r_job(1, 1))
        squash(0, 0)
        squash(1, 0)
        empty(r_job(1, 0))
        empty(r_job(1, 1))
        squash(2, 0)
        squash(3, 0)
        weigh_next((0, 0))
        weigh_next((1, 0))
        quantise(r_job(1, 0))
        quantise(r_job(1, 1))
        metric_passes(1, 1)
        metric_passes(2, 1)
        shape_pass(0, 1)
        shape_pass(1, 1)
        shape_pass(2, 1)
        split_r(2)
        split_fp(4)
        weigh_next((2, 0))
        weigh_next((3, 0))

        step(
            [r_job(2, 0), r_job(2, 1), fp_job(4, 0), fp_job(4, 1), y_job((0, 0), (1, 0))],
            [(0, 1), (1, 1), (2, 1)], [(3, 1), (0, 2), (1, 2), (2, 2)], [(split_sh, 2), (split_fp, 5)],
        )
        step(
            [sh_job(2), fp_job(5, 0), fp_job(5, 1), y_job((2, 0), (3, 0)), y_job((0, 1), (1, 1))],
            [(2, 2)], [(3, 2), (4, 0), (4, 1)], [(split_fp, 6), (split_sh, 3)],
            [lambda: store_codes(0, 4, slice(0, 1))],
        )
        step(
            [fp_job(6, 0), fp_job(6, 1), sh_job(3), y_job((2, 1), (3, 1)), y_job((0, 2), (1, 2))],
            [(4, 1)], [(5, 0), (5, 1)], [(split_fp, 7)],
            [lambda: store_codes(0, 4, slice(1, 2))],
        )
        step(
            [fp_job(7, 0), fp_job(7, 1), y_job((2, 2), (3, 2)), y_job((4, 0), (4, 1))],
            [(5, 1)], [(6, 0), (6, 1), (7, 0), (7, 1), (4, 2)], [],
            [lambda: store_codes(0, 4, slice(2, 3))],
        )
        step(
            [y_job((5, 0), (5, 1)), y_job((6, 0), (7, 0)), y_job((6, 1), (7, 1))],
            [(4, 2)], [(5, 2), (6, 2)], [],
            [lambda: store_codes(4, 8, slice(0, 2)), lambda: store_scales(slice(0, 2), [nc.sync] * 4)],
        )
        t, c = TILES - 1, CHUNKS - 1
        squash(t - 1, c)
        weigh(t - 1, c)
        squashed[t, c] = work.tile([P, CHUNK], F32, tag="squashed", name="squashed", bufs=4)
        y_last = work.tile([P, 2, P, 2], BF16, tag="y_bf", bufs=10)
        halves["y", t, c] = [y_last[:, u, :, :].rearrange("p c e -> p (c e)").bitcast(F32) for u in range(2)]
        for q in range(4):
            last_unit_quarter(t, c, q)
            part = squashed[t, c][:, q * P : (q + 1) * P]
            nc.scalar.activation(out=part, in_=acc[t, c, q][:], func=TANH, scale=inv_cols[:, t : t + 1])
            give_bank((t, c, q))
            nc.vector.tensor_tensor(
                out=y_last[:, :, 32 * q : 32 * (q + 1), :],
                in0=part.rearrange("p (c u e) -> p u c e", u=2, e=2),
                in1=w_rows[:, c * CHUNK + q * P : c * CHUNK + (q + 1) * P].rearrange("p (c u e) -> p u c e", u=2, e=2),
                op=MULT,
            )
            if q == 1:
                round_y(t - 1, c)
        early, mid, late = y_job((t - 3, c), (t - 2, c)), y_job((t - 1, c)), y_job((t, c))
        turn(early, mid, late)
        weigh(t, c)
        stage(early, mid)
        store_codes(t - 3, t, slice(2, 3))
        stage(late)
        store_codes(t, t + 1, slice(2, 3))
        store_scales(slice(2, 3), [nc.scalar, nc.scalar, nc.sync, nc.sync])
